import numpy as np
import ml_dtypes


def mxq(x, axis, fmt="e4m3"):
    dtype, down = {"e4m3": (ml_dtypes.float8_e4m3fn, 7), "e5m2": (ml_dtypes.float8_e5m2, 14)}[fmt]
    v = np.moveaxis(np.asarray(x, np.float32).astype(ml_dtypes.bfloat16).astype(np.float64), axis, -1)
    blocks = v.reshape(v.shape[:-1] + (-1, 32))
    amax = np.abs(blocks).max(-1, keepdims=True)
    byte = np.maximum(np.where(amax > 0, np.frexp(amax)[1] - 1 + 127, 0) - down, 1)
    scale = np.exp2(byte - 127.0)
    codes = (blocks / scale).astype(np.float32).astype(dtype).astype(np.float64)
    return np.moveaxis((codes * scale).reshape(v.shape), -1, axis)


WIDE = False


def mx_kscale(k):
    if not WIDE:
        return np.ones(k)
    levels = np.array([10, -10, 5, -5, 0])
    if k % 512:
        return np.exp2(np.random.permutation(np.resize(levels, k // 32))).repeat(32)
    a = np.empty((k // 512, 16))
    for p in range(k // 512):
        a[p, :8] = np.random.permutation(np.resize(levels, 8))
        for g in range(8):
            far = levels[np.abs(levels - a[p, g]) >= 10]
            a[p, g + 8] = far[np.random.randint(len(far))]
    return np.exp2(a.ravel()).repeat(32)


def f64(x):
    return np.asarray(x).astype(np.float64)


def striped(idx):
    return np.tile(idx.reshape(-1, 16).T, (8, 1)).astype(np.uint16)


def unstriped(offs):
    return offs[:16].T.reshape(-1).astype(np.int64)


E2M1 = np.array([0.0, 0.5, 1.0, 1.5, 2.0, 3.0, 4.0, 6.0, -0.0, -0.5, -1.0, -1.5, -2.0, -3.0, -4.0, -6.0])


def pack_weight(w, fmt):
    k, n = w.shape
    w = f64(np.asarray(w, np.float32).astype(ml_dtypes.bfloat16)).reshape(k // 32, 32, n)
    amax = np.abs(w).max(1)
    if fmt == "e4m3":
        byte = np.frexp(amax)[1] - 1 + 127 - 7
    else:
        mant, ex = np.frexp(amax / 6.0)
        byte = np.where(mant > 0.5, ex, ex - 1) + 127
    byte = np.clip(np.where(amax > 0, byte, 1), 1, 254)
    scaled = (w * np.exp2(127.0 - byte)[:, None, :]).reshape(k, n).astype(np.float32)
    by_word = np.ascontiguousarray(scaled.reshape(k // 512, 128, 4, n).transpose(0, 1, 3, 2))
    if fmt == "e4m3":
        words = by_word.astype(ml_dtypes.float8_e4m3fn).view(np.uint8)
    else:
        c = by_word.astype(ml_dtypes.float4_e2m1fn).view(np.uint8) & 0xF
        words = (c[..., 0::2] | (c[..., 1::2] << 4)).reshape(k // 512, 128, 2 * n)
    return np.ascontiguousarray(words), np.ascontiguousarray(byte.astype(np.uint8).reshape(k // 512, 16, n))


def unpack_weight(words, scales, fmt):
    g, _, n = scales.shape
    words = np.ascontiguousarray(words).reshape(g, 128, n, -1)
    if fmt == "e4m3":
        vals = words.view(ml_dtypes.float8_e4m3fn).astype(np.float64)
    else:
        nib = np.empty((g, 128, n, 4), np.uint8)
        nib[..., 0::2] = words & 0xF
        nib[..., 1::2] = words >> 4
        vals = E2M1[nib]
    vals = vals * np.repeat(np.exp2(scales.astype(np.float64) - 127.0), 8, axis=1)[..., None]
    return vals.transpose(0, 1, 3, 2).reshape(g * 512, n)


def gelu(v):
    return 0.5 * v * (1.0 + np.tanh(np.sqrt(2.0 / np.pi) * (v + 0.044715 * v**3)))


K, K2, H, N, T, S = 1024, 512, 1024, 640, 4096, 1024

def setup_inputs():
    n = np.random.standard_normal
    s = mx_kscale(K)[:, None]
    s2 = mx_kscale(K2)[:, None]
    u = mx_kscale(H)[:, None]
    d = {}
    d["tab_words"], d["tab_scales"] = pack_weight(n((K, T)) * s, "e4m3")
    d["offs"] = striped(np.random.permutation(T)[:S])
    d["xs_words"], d["xs_scales"] = pack_weight(n((K2, S)) * s2, "e4m3")
    d["wcut"] = (1.3 * n((K, H)) / K**0.5 / s).astype(np.float32)
    d["bcut"] = (0.5 * n(H)).astype(np.float32)
    d["wscan_words"], d["wscan_scales"] = pack_weight(n((K2, H)) / K2**0.5 / s2 * u.T, "e2m1")
    d["bscan"] = (0.5 * n(H) * u[:, 0]).astype(np.float32)
    d["wret"] = (1.3 * n((H, N)) / H**0.5 / u).astype(np.float32)
    d["wref_words"], d["wref_scales"] = pack_weight(0.8 * n((H, N)) / H**0.5 / u, "e4m3")
    return d

def reference(tab_words, tab_scales, offs, xs_words, xs_scales, wcut, bcut,
              wscan_words, wscan_scales, bscan, wret, wref_words, wref_scales):
    v = unpack_weight(tab_words, tab_scales, "e4m3")[:, unstriped(offs)]
    xs = unpack_weight(xs_words, xs_scales, "e4m3")
    wscan = unpack_weight(wscan_words, wscan_scales, "e2m1")
    wref = unpack_weight(wref_words, wref_scales, "e4m3")
    cut = np.tanh((mxq(f64(wcut), 0, "e4m3").T @ v) + f64(bcut)[:, None])
    b = np.abs((wscan.T @ xs) + f64(bscan)[:, None])
    h = cut * b
    ret = mxq(f64(wret), 0, "e4m3").T @ mxq(h, 0, "e4m3")
    ref = wref.T @ mxq(b, 0, "e4m3")
    return np.abs(ret - ref)

@@ -1,0 +1,261 @@
+from contextlib import ExitStack
+
+import concourse.mybir as mybir
+
+K, K2, H, N, T, S = 1024, 512, 1024, 640, 4096, 1024
+FLOPS = 2 * S * (K * H + K2 * H + 2 * H * N)
+
+F32 = mybir.dt.float32
+BF16 = mybir.dt.bfloat16
+I32 = mybir.dt.int32
+U32 = mybir.dt.uint32
+U16 = mybir.dt.uint16
+U8 = mybir.dt.uint8
+E4M3 = mybir.dt.float8_e4m3fn_x4
+E2M1 = mybir.dt.float4_e2m1fn_x4
+ACT = mybir.ActivationFunctionType
+ALU = mybir.AluOpType
+
+P = 128
+PACK = 4
+PASS = P * PACK
+COLS = 512
+QUADS = 4
+BANKS = 8
+
+
+def tile_list_light_return_audit_kernel(
+    tc, tab_words, tab_scales, offs, xs_words, xs_scales, wcut, bcut,
+    wscan_words, wscan_scales, bscan, wret, wref_words, wref_scales, out,
+):
+    nc = tc.nc
+    k_passes, r_passes, halves, n_tiles = K // PASS, H // PASS, S // COLS, N // P
+
+    with ExitStack() as ctx:
+        held = ctx.enter_context(tc.tile_pool(name="held", bufs=1))
+        ring = ctx.enter_context(tc.tile_pool(name="ring", bufs=2))
+        stores = ctx.enter_context(tc.tile_pool(name="stores", bufs=5))
+        psum = ctx.enter_context(tc.psum_pool(name="psum", bufs=1))
+
+        def keep(name, width, dtype):
+            return held.tile([P, width], dtype, name=name, align_bytes=64)
+
+        banks = [psum.tile([P, COLS], F32, name="bank%d" % i) for i in range(BANKS)]
+        offsets = held.tile([P, S // 16], U16, name="offsets")
+
+        def load_words(tile, words):
+            nc.sync.dma_start(tile[:].bitcast(I32), words.rearrange("p n t -> p (n t)").bitcast(I32))
+
+        def load_planes(queue, tile, scales):
+            passes = scales.shape[0]
+            for q in range(QUADS):
+                queue.dma_start(
+                    tile[32 * q : 32 * q + 4 * passes, :].bitcast(I32),
+                    scales[:, 4 * q : 4 * q + 4, :].bitcast(I32),
+                )
+
+        def load_rows(name, rows):
+            raw = held.tile([P, PACK, rows.shape[1]], F32, name=name, align_bytes=64)
+            nc.sync.dma_start(raw[:], rows.rearrange("(p j) c -> p j c", j=PACK))
+            return raw
+
+        def load_bias(queue, name, vec):
+            tile = held.tile([P, r_passes, PACK], F32, name=name, align_bytes=64)
+            queue.dma_start(tile[:], vec.rearrange("(b p t) -> p b t", b=r_passes, t=PACK))
+            return tile
+
+        wscan_raw = keep("wscan_raw", 2 * H, U8)
+        wscan_plane_raw = keep("wscan_plane_raw", H, U8)
+        xs_codes = keep("xs_codes", S, U32)
+        xs_plane = keep("xs_plane", S, U8)
+        tab_codes = [keep("tab_codes%d" % a, T, U32) for a in range(k_passes)]
+        tab_planes = keep("tab_planes", T, U8)
+        wref_codes = [keep("wref_codes%d" % b, N, U32) for b in range(r_passes)]
+        wref_planes = keep("wref_planes", N, U8)
+
+        for plane in (wscan_plane_raw, xs_plane):
+            nc.gpsimd.memset(plane[:].bitcast(I32), 0)
+        for plane in (tab_planes, wref_planes):
+            nc.vector.memset(plane[:].bitcast(I32), 0)
+
+        warm_in = keep("warm_in", 1, F32)
+        warm_out = keep("warm_out", 1, F32)
+        nc.vector.memset(warm_in[:], 0.0)
+        nc.scalar.activation(warm_out[:], warm_in[:], ACT.Tanh)
+
+        def wcut_rows(a, b):
+            return wcut[a * PASS : (a + 1) * PASS, b * PASS : (b + 1) * PASS]
+
+        wcut_raw = {}
+        nc.sync.dma_start(wscan_raw[:].bitcast(I32), wscan_words[0].bitcast(I32))
+        load_words(xs_codes, xs_words[0])
+        load_planes(nc.sync, wscan_plane_raw, wscan_scales)
+        load_planes(nc.sync, xs_plane, xs_scales)
+        bscan_t = load_bias(nc.sync, "bscan_t", bscan)
+        wcut_raw[0, 0] = load_rows("wcut_raw00", wcut_rows(0, 0))
+        load_words(tab_codes[0], tab_words[0])
+        load_planes(nc.sync, tab_planes, tab_scales)
+        nc.sync.dma_start(offsets[:], offs)
+        wcut_raw[1, 0] = load_rows("wcut_raw10", wcut_rows(1, 0))
+        load_words(tab_codes[1], tab_words[1])
+        bcut_t = load_bias(nc.sync, "bcut_t", bcut)
+        for a in range(k_passes):
+            wcut_raw[a, 1] = load_rows("wcut_raw%d1" % a, wcut_rows(a, 1))
+        load_planes(nc.sync, wref_planes, wref_scales)
+        wret_raw = []
+        for b in range(r_passes):
+            load_words(wref_codes[b], wref_words[b])
+            wret_raw.append(load_rows("wret_raw%d" % b, wret[b * PASS : (b + 1) * PASS, :]))
+
+        def quantise(name, staged, width):
+            codes = keep(name + "_codes", width, U32)
+            plane = keep(name + "_plane", width, U8)
+            for c0 in range(0, width, COLS):
+                c1 = min(c0 + COLS, width)
+                nc.vector.quantize_mx(
+                    out=codes[:, c0:c1].bitcast(E4M3), scales=plane[:, c0:c1],
+                    in_=staged[:, PACK * c0 : PACK * c1],
+                )
+            return codes, plane
+
+        def woven(staged):
+            return staged.rearrange("p (c i t) -> p c t i", i=4, t=PACK)
+
+        def by_fours(slices):
+            return slices.rearrange("p t (c i) -> p c t i", i=4)
+
+        def prepare_wcut(a, b, on_scalar):
+            staged = ring.tile([P, PACK * N], BF16, name="w_staged", align_bytes=64)
+            dst = staged[:, : PACK * PASS].rearrange("p (t m j) -> p m j t", t=PACK, j=PACK)
+            src = wcut_raw[a, b][:].rearrange("p j (m t) -> p m j t", t=PACK)
+            if on_scalar:
+                nc.scalar.copy(dst, src)
+            else:
+                nc.vector.tensor_copy(dst, src)
+            return quantise("wcut%d%d" % (a, b), staged, PASS)
+
+        def prepare_wret(b, on_scalar):
+            staged = ring.tile([P, PACK * N], BF16, name="w_staged", align_bytes=64)
+            if on_scalar:
+                nc.scalar.activation(woven(staged[:]), by_fours(wret_raw[b][:]), ACT.Copy, scale=-1.0)
+            else:
+                nc.vector.tensor_scalar_mul(woven(staged[:]), by_fours(wret_raw[b][:]), -1.0)
+            return quantise("wret%d" % b, staged, N)
+
+        wcut_q = {}
+        wcut_q[0, 0] = prepare_wcut(0, 0, True)
+
+        wscan_codes, wscan_plane = [], []
+        for b in range(r_passes):
+            codes = keep("wscan_codes%d" % b, 2 * PASS, U8)
+            plane = keep("wscan_plane%d" % b, PASS, U8)
+            nc.vector.tensor_copy(
+                codes[:].rearrange("p (t m e) -> p t m e", t=PACK, e=2),
+                wscan_raw[:, 2 * PASS * b : 2 * PASS * (b + 1)].rearrange("p (m t e) -> p t m e", t=PACK, e=2),
+            )
+            nc.vector.tensor_copy(
+                plane[:].rearrange("p (t m) -> p t m", t=PACK),
+                wscan_plane_raw[:, PASS * b : PASS * (b + 1)].rearrange("p (m t) -> p t m", t=PACK),
+            )
+            wscan_codes.append(codes)
+            wscan_plane.append(plane)
+
+        def gather(name, window, dtype, half):
+            picked = keep(name, COLS, dtype)
+            cols = slice(half * COLS // 16, (half + 1) * COLS // 16)
+            nc.vector.tensor_copy(picked[:], window[:].indirect(offsets[:, cols]))
+            return picked
+
+        b_f32, b_q = {}, {}
+
+        def scan_response(b, half, first_bank):
+            cols = slice(half * COLS, (half + 1) * COLS)
+            vals = held.tile([P, PACK, COLS], F32, name="b_f32_%d%d" % (b, half), align_bytes=64)
+            for t in range(PACK):
+                bank = banks[first_bank + t]
+                nc.tensor.matmul_mx(
+                    out=bank[:],
+                    lhsT=wscan_codes[b][:, 2 * P * t : 2 * P * (t + 1)].bitcast(E2M1),
+                    lhsT_scale=wscan_plane[b][:, P * t : P * (t + 1)],
+                    rhs=xs_codes[:, cols].bitcast(E4M3), rhs_scale=xs_plane[:, cols],
+                    start=True, stop=True,
+                )
+                nc.scalar.activation(vals[:, t, :], bank[:], ACT.Abs, bias=bscan_t[:, b, t : t + 1])
+            b_f32[b, half] = vals
+
+        def quantise_b(b, half):
+            staged = ring.tile([P, PACK * COLS], BF16, name="a_staged", align_bytes=64)
+            nc.vector.tensor_copy(woven(staged[:]), by_fours(b_f32[b, half][:]))
+            b_q[b, half] = quantise("b%d%d" % (b, half), staged, COLS)
+
+        steps = [(b, half) for b in range(r_passes) for half in range(halves)]
+        for i, (b, half) in enumerate(steps):
+            scan_response(b, half, PACK * (i % 2))
+
+        v_planes = [gather("v_planes%d" % half, tab_planes, U8, half) for half in range(halves)]
+        v_codes = {}
+        for half in range(halves):
+            v_codes[0, half] = gather("v_codes0%d" % half, tab_codes[0], U32, half)
+        wcut_q[1, 0] = prepare_wcut(1, 0, True)
+        for half in range(halves):
+            v_codes[1, half] = gather("v_codes1%d" % half, tab_codes[1], U32, half)
+        for b, half in steps:
+            quantise_b(b, half)
+
+        h_q = {}
+
+        def cut_features(b, half, bank_of):
+            cut = ring.tile([P, PACK, COLS], F32, name="cut", align_bytes=64)
+            for t in range(PACK):
+                bank = banks[bank_of(t)]
+                cols = slice(P * t, P * (t + 1))
+                for a in range(k_passes):
+                    codes, plane = wcut_q[a, b]
+                    nc.tensor.matmul_mx(
+                        out=bank[:],
+                        lhsT=codes[:, cols].bitcast(E4M3), lhsT_scale=plane[:, cols],
+                        rhs=v_codes[a, half][:].bitcast(E4M3), rhs_scale=v_planes[half][4 * a :, :],
+                        start=(a == 0), stop=(a == k_passes - 1),
+                    )
+                nc.scalar.activation(cut[:, t, :], bank[:], ACT.Tanh, bias=bcut_t[:, b, t : t + 1])
+            staged = ring.tile([P, PACK * COLS], BF16, name="a_staged", align_bytes=64)
+            nc.vector.tensor_tensor(woven(staged[:]), by_fours(cut[:]), by_fours(b_f32[b, half][:]), ALU.mult)
+            h_q[b, half] = quantise("h%d%d" % (b, half), staged, COLS)
+
+        wret_q = {}
+        cut_features(0, 0, lambda t: t)
+        wcut_q[0, 1] = prepare_wcut(0, 1, True)
+        wcut_q[1, 1] = prepare_wcut(1, 1, False)
+        cut_features(0, 1, lambda t: PACK + t)
+        cut_features(1, 0, lambda t: t % 3)
+        wret_q[0] = prepare_wret(0, True)
+        cut_features(1, 1, lambda t: (PACK + t) % 3)
+        wret_q[1] = prepare_wret(1, False)
+
+        def readings(half, bank_order):
+            for nt in range(n_tiles):
+                bank = banks[bank_order[nt]]
+                cols = slice(P * nt, P * (nt + 1))
+                for b in range(r_passes):
+                    codes, plane = b_q[b, half]
+                    nc.tensor.matmul_mx(
+                        out=bank[:],
+                        lhsT=wref_codes[b][:, cols].bitcast(E4M3), lhsT_scale=wref_planes[4 * b :, cols],
+                        rhs=codes[:].bitcast(E4M3), rhs_scale=plane[:],
+                        start=(b == 0), stop=False,
+                    )
+                for b in range(r_passes):
+                    codes, plane = h_q[b, half]
+                    w_codes, w_plane = wret_q[b]
+                    nc.tensor.matmul_mx(
+                        out=bank[:],
+                        lhsT=w_codes[:, cols].bitcast(E4M3), lhsT_scale=w_plane[:, cols],
+                        rhs=codes[:].bitcast(E4M3), rhs_scale=plane[:],
+                        start=False, stop=(b == r_passes - 1),
+                    )
+                result = stores.tile([P, COLS], F32, name="result")
+                nc.scalar.activation(result[:], bank[:], ACT.Abs)
+                nc.sync.dma_start(out[cols, half * COLS : (half + 1) * COLS], result[:])
+
+        readings(0, [3, 4, 5, 6, 7])
+        readings(1, [2, 0, 1, 3, 4])

@@ -19,9 +19,12 @@ ALU = mybir.AluOpType
 P = 128
 PACK = 4
 PASS = P * PACK
-COLS = 512
 QUADS = 4
+HALF = 512
+QUARTER = HALF // 2
 BANKS = 8
+LINE = 4
+LIST_ROWS = 16
 
 
 def tile_list_light_return_audit_kernel(
@@ -29,27 +32,28 @@ def tile_list_light_return_audit_kernel(
     wscan_words, wscan_scales, bscan, wret, wref_words, wref_scales, out,
 ):
     nc = tc.nc
-    k_passes, r_passes, halves, n_tiles = K // PASS, H // PASS, S // COLS, N // P
+    k_passes, r_blocks, halves, n_tiles = K // PASS, H // PASS, S // HALF, N // P
 
     with ExitStack() as ctx:
         held = ctx.enter_context(tc.tile_pool(name="held", bufs=1))
         ring = ctx.enter_context(tc.tile_pool(name="ring", bufs=2))
-        stores = ctx.enter_context(tc.tile_pool(name="stores", bufs=5))
         psum = ctx.enter_context(tc.psum_pool(name="psum", bufs=1))
 
         def keep(name, width, dtype):
             return held.tile([P, width], dtype, name=name, align_bytes=64)
 
-        banks = [psum.tile([P, COLS], F32, name="bank%d" % i) for i in range(BANKS)]
-        offsets = held.tile([P, S // 16], U16, name="offsets")
+        banks = [psum.tile([P, HALF], F32, name="bank%d" % i) for i in range(BANKS)]
+        offsets = held.tile([P, S // LIST_ROWS], U16, name="offsets")
 
-        def load_words(tile, words):
+        def load_words(name, words):
+            tile = keep(name, words.shape[1], U32)
             nc.sync.dma_start(tile[:].bitcast(I32), words.rearrange("p n t -> p (n t)").bitcast(I32))
+            return tile
 
-        def load_planes(queue, tile, scales):
+        def load_planes(tile, scales):
             passes = scales.shape[0]
             for q in range(QUADS):
-                queue.dma_start(
+                nc.sync.dma_start(
                     tile[32 * q : 32 * q + 4 * passes, :].bitcast(I32),
                     scales[:, 4 * q : 4 * q + 4, :].bitcast(I32),
                 )
@@ -59,23 +63,20 @@ def tile_list_light_return_audit_kernel(
             nc.sync.dma_start(raw[:], rows.rearrange("(p j) c -> p j c", j=PACK))
             return raw
 
-        def load_bias(queue, name, vec):
-            tile = held.tile([P, r_passes, PACK], F32, name=name, align_bytes=64)
-            queue.dma_start(tile[:], vec.rearrange("(b p t) -> p b t", b=r_passes, t=PACK))
+        def load_wcut(a, b):
+            return load_rows("wcut_raw%d%d" % (a, b), wcut[a * PASS : (a + 1) * PASS, b * PASS : (b + 1) * PASS])
+
+        def load_bias(name, vec):
+            tile = held.tile([P, r_blocks, PACK], F32, name=name, align_bytes=64)
+            nc.sync.dma_start(tile[:], vec.rearrange("(b p t) -> p b t", b=r_blocks, t=PACK))
             return tile
 
-        wscan_raw = keep("wscan_raw", 2 * H, U8)
         wscan_plane_raw = keep("wscan_plane_raw", H, U8)
-        xs_codes = keep("xs_codes", S, U32)
         xs_plane = keep("xs_plane", S, U8)
-        tab_codes = [keep("tab_codes%d" % a, T, U32) for a in range(k_passes)]
         tab_planes = keep("tab_planes", T, U8)
-        wref_codes = [keep("wref_codes%d" % b, N, U32) for b in range(r_passes)]
         wref_planes = keep("wref_planes", N, U8)
-
-        for plane in (wscan_plane_raw, xs_plane):
-            nc.gpsimd.memset(plane[:].bitcast(I32), 0)
-        for plane in (tab_planes, wref_planes):
+        nc.gpsimd.memset(wscan_plane_raw[:].bitcast(I32), 0)
+        for plane in (xs_plane, tab_planes, wref_planes):
             nc.vector.memset(plane[:].bitcast(I32), 0)
 
         warm_in = keep("warm_in", 1, F32)
@@ -83,35 +84,30 @@ def tile_list_light_return_audit_kernel(
         nc.vector.memset(warm_in[:], 0.0)
         nc.scalar.activation(warm_out[:], warm_in[:], ACT.Tanh)
 
-        def wcut_rows(a, b):
-            return wcut[a * PASS : (a + 1) * PASS, b * PASS : (b + 1) * PASS]
-
-        wcut_raw = {}
+        wscan_raw = keep("wscan_raw", 2 * H, U8)
         nc.sync.dma_start(wscan_raw[:].bitcast(I32), wscan_words[0].bitcast(I32))
-        load_words(xs_codes, xs_words[0])
-        load_planes(nc.sync, wscan_plane_raw, wscan_scales)
-        load_planes(nc.sync, xs_plane, xs_scales)
-        bscan_t = load_bias(nc.sync, "bscan_t", bscan)
-        wcut_raw[0, 0] = load_rows("wcut_raw00", wcut_rows(0, 0))
-        load_words(tab_codes[0], tab_words[0])
-        load_planes(nc.sync, tab_planes, tab_scales)
+        load_planes(wscan_plane_raw, wscan_scales)
+        xs_codes = load_words("xs_codes", xs_words[0])
+        load_planes(xs_plane, xs_scales)
+        bscan_rows = load_bias("bscan_rows", bscan)
+        wcut_raw = {(0, 0): load_wcut(0, 0)}
+        load_planes(tab_planes, tab_scales)
         nc.sync.dma_start(offsets[:], offs)
-        wcut_raw[1, 0] = load_rows("wcut_raw10", wcut_rows(1, 0))
-        load_words(tab_codes[1], tab_words[1])
-        bcut_t = load_bias(nc.sync, "bcut_t", bcut)
+        tab_codes = [load_words("tab_codes0", tab_words[0])]
+        wcut_raw[1, 0] = load_wcut(1, 0)
+        tab_codes.append(load_words("tab_codes1", tab_words[1]))
+        bcut_rows = load_bias("bcut_rows", bcut)
         for a in range(k_passes):
-            wcut_raw[a, 1] = load_rows("wcut_raw%d1" % a, wcut_rows(a, 1))
-        load_planes(nc.sync, wref_planes, wref_scales)
-        wret_raw = []
-        for b in range(r_passes):
-            load_words(wref_codes[b], wref_words[b])
-            wret_raw.append(load_rows("wret_raw%d" % b, wret[b * PASS : (b + 1) * PASS, :]))
+            wcut_raw[a, 1] = load_wcut(a, 1)
+        load_planes(wref_planes, wref_scales)
+        wref_codes = [load_words("wref_codes%d" % b, wref_words[b]) for b in range(r_blocks)]
+        wret_raw = [load_rows("wret_raw%d" % b, wret[b * PASS : (b + 1) * PASS, :]) for b in range(r_blocks)]
 
         def quantise(name, staged, width):
             codes = keep(name + "_codes", width, U32)
             plane = keep(name + "_plane", width, U8)
-            for c0 in range(0, width, COLS):
-                c1 = min(c0 + COLS, width)
+            for c0 in range(0, width, HALF):
+                c1 = min(c0 + HALF, width)
                 nc.vector.quantize_mx(
                     out=codes[:, c0:c1].bitcast(E4M3), scales=plane[:, c0:c1],
                     in_=staged[:, PACK * c0 : PACK * c1],
@@ -119,34 +115,31 @@ def tile_list_light_return_audit_kernel(
             return codes, plane
 
         def woven(staged):
-            return staged.rearrange("p (c i t) -> p c t i", i=4, t=PACK)
+            return staged.rearrange("p (c i t) -> p c t i", i=LINE, t=PACK)
 
-        def by_fours(slices):
-            return slices.rearrange("p t (c i) -> p c t i", i=4)
+        def by_lines(slices):
+            return slices.rearrange("p t (c i) -> p c t i", i=LINE)
 
-        def prepare_wcut(a, b, on_scalar):
-            staged = ring.tile([P, PACK * N], BF16, name="w_staged", align_bytes=64)
-            dst = staged[:, : PACK * PASS].rearrange("p (t m j) -> p m j t", t=PACK, j=PACK)
-            src = wcut_raw[a, b][:].rearrange("p j (m t) -> p m j t", t=PACK)
-            if on_scalar:
-                nc.scalar.copy(dst, src)
-            else:
-                nc.vector.tensor_copy(dst, src)
+        def prepare_wcut(a, b, copy):
+            staged = ring.tile([P, PACK * PASS], BF16, name="wcut_staged", align_bytes=64)
+            copy(
+                staged[:].rearrange("p (t m j) -> p m j t", t=PACK, j=PACK),
+                wcut_raw[a, b][:].rearrange("p j (m t) -> p m j t", t=PACK),
+            )
             return quantise("wcut%d%d" % (a, b), staged, PASS)
 
-        def prepare_wret(b, on_scalar):
-            staged = ring.tile([P, PACK * N], BF16, name="w_staged", align_bytes=64)
-            if on_scalar:
-                nc.scalar.activation(woven(staged[:]), by_fours(wret_raw[b][:]), ACT.Copy, scale=-1.0)
-            else:
-                nc.vector.tensor_scalar_mul(woven(staged[:]), by_fours(wret_raw[b][:]), -1.0)
+        def prepare_wret(b):
+            staged = keep("wret_staged%d" % b, PACK * N, BF16)
+            nc.vector.tensor_scalar_mul(woven(staged[:]), by_lines(wret_raw[b][:]), -1.0)
             return quantise("wret%d" % b, staged, N)
 
-        wcut_q = {}
-        wcut_q[0, 0] = prepare_wcut(0, 0, True)
+        def values_staged():
+            return ring.tile([P, PACK * HALF], BF16, name="values_staged", align_bytes=64)
+
+        wcut_mx = {(0, 0): prepare_wcut(0, 0, nc.vector.tensor_copy)}
 
         wscan_codes, wscan_plane = [], []
-        for b in range(r_passes):
+        for b in range(r_blocks):
             codes = keep("wscan_codes%d" % b, 2 * PASS, U8)
             plane = keep("wscan_plane%d" % b, PASS, U8)
             nc.vector.tensor_copy(
@@ -160,102 +153,123 @@ def tile_list_light_return_audit_kernel(
             wscan_codes.append(codes)
             wscan_plane.append(plane)
 
-        def gather(name, window, dtype, half):
-            picked = keep(name, COLS, dtype)
-            cols = slice(half * COLS // 16, (half + 1) * COLS // 16)
-            nc.vector.tensor_copy(picked[:], window[:].indirect(offsets[:, cols]))
-            return picked
+        response, response_mx = {}, {}
 
-        b_f32, b_q = {}, {}
-
-        def scan_response(b, half, first_bank):
-            cols = slice(half * COLS, (half + 1) * COLS)
-            vals = held.tile([P, PACK, COLS], F32, name="b_f32_%d%d" % (b, half), align_bytes=64)
+        def scan_response(b, half):
+            tokens = slice(half * HALF, (half + 1) * HALF)
+            values = held.tile([P, PACK, HALF], F32, name="response%d%d" % (b, half), align_bytes=64)
             for t in range(PACK):
-                bank = banks[first_bank + t]
+                bank = banks[PACK * half + t]
                 nc.tensor.matmul_mx(
                     out=bank[:],
                     lhsT=wscan_codes[b][:, 2 * P * t : 2 * P * (t + 1)].bitcast(E2M1),
                     lhsT_scale=wscan_plane[b][:, P * t : P * (t + 1)],
-                    rhs=xs_codes[:, cols].bitcast(E4M3), rhs_scale=xs_plane[:, cols],
+                    rhs=xs_codes[:, tokens].bitcast(E4M3), rhs_scale=xs_plane[:, tokens],
                     start=True, stop=True,
                 )
-                nc.scalar.activation(vals[:, t, :], bank[:], ACT.Abs, bias=bscan_t[:, b, t : t + 1])
-            b_f32[b, half] = vals
+                nc.scalar.activation(values[:, t, :], bank[:], ACT.Abs, bias=bscan_rows[:, b, t : t + 1])
+            response[b, half] = values
 
-        def quantise_b(b, half):
-            staged = ring.tile([P, PACK * COLS], BF16, name="a_staged", align_bytes=64)
-            nc.vector.tensor_copy(woven(staged[:]), by_fours(b_f32[b, half][:]))
-            b_q[b, half] = quantise("b%d%d" % (b, half), staged, COLS)
+        def quantise_response(b, half, staged, copy):
+            copy(woven(staged[:]), by_lines(response[b, half][:]))
+            response_mx[b, half] = quantise("response%d%d" % (b, half), staged, HALF)
 
-        steps = [(b, half) for b in range(r_passes) for half in range(halves)]
-        for i, (b, half) in enumerate(steps):
-            scan_response(b, half, PACK * (i % 2))
-
-        v_planes = [gather("v_planes%d" % half, tab_planes, U8, half) for half in range(halves)]
-        v_codes = {}
         for half in range(halves):
-            v_codes[0, half] = gather("v_codes0%d" % half, tab_codes[0], U32, half)
-        wcut_q[1, 0] = prepare_wcut(1, 0, True)
+            scan_response(0, half)
+        wcut_mx[1, 0] = prepare_wcut(1, 0, nc.scalar.copy)
         for half in range(halves):
-            v_codes[1, half] = gather("v_codes1%d" % half, tab_codes[1], U32, half)
-        for b, half in steps:
-            quantise_b(b, half)
+            scan_response(1, half)
 
-        h_q = {}
+        def gather(name, window, dtype, piece):
+            picked = keep(name, S, dtype)
+            for j0 in range(0, S, piece):
+                entries = offsets[:, j0 // LIST_ROWS : (j0 + piece) // LIST_ROWS]
+                nc.vector.tensor_copy(picked[:, j0 : j0 + piece], window[:].indirect(entries))
+            return picked
 
-        def cut_features(b, half, bank_of):
-            cut = ring.tile([P, PACK, COLS], F32, name="cut", align_bytes=64)
+        v_planes = gather("v_planes", tab_planes, U8, S)
+        v_codes = [gather("v_codes0", tab_codes[0], U32, S), gather("v_codes1", tab_codes[1], U32, HALF)]
+
+        for half in range(halves):
+            quantise_response(0, half, values_staged(), nc.vector.tensor_copy)
+        quantise_response(1, 0, values_staged(), nc.scalar.copy)
+        last_staged = held.tile([P, PACK * HALF], BF16, name="last_staged", tag="tab_codes1", align_bytes=64)
+        quantise_response(1, 1, last_staged, nc.vector.tensor_copy)
+
+        h_mx = {}
+
+        def cut_features(b, half, bank_order, home, piece):
+            tokens = slice(half * HALF, (half + 1) * HALF)
+            cut = held.tile([P, PACK, HALF], F32, name="cut%d%d" % (b, half), tag=home, align_bytes=64)
             for t in range(PACK):
-                bank = banks[bank_of(t)]
-                cols = slice(P * t, P * (t + 1))
+                bank = banks[bank_order[t]]
+                columns = slice(P * t, P * (t + 1))
                 for a in range(k_passes):
-                    codes, plane = wcut_q[a, b]
+                    codes, plane = wcut_mx[a, b]
                     nc.tensor.matmul_mx(
                         out=bank[:],
-                        lhsT=codes[:, cols].bitcast(E4M3), lhsT_scale=plane[:, cols],
-                        rhs=v_codes[a, half][:].bitcast(E4M3), rhs_scale=v_planes[half][4 * a :, :],
+                        lhsT=codes[:, columns].bitcast(E4M3), lhsT_scale=plane[:, columns],
+                        rhs=v_codes[a][:, tokens].bitcast(E4M3), rhs_scale=v_planes[4 * a :, tokens],
                         start=(a == 0), stop=(a == k_passes - 1),
                     )
-                nc.scalar.activation(cut[:, t, :], bank[:], ACT.Tanh, bias=bcut_t[:, b, t : t + 1])
-            staged = ring.tile([P, PACK * COLS], BF16, name="a_staged", align_bytes=64)
-            nc.vector.tensor_tensor(woven(staged[:]), by_fours(cut[:]), by_fours(b_f32[b, half][:]), ALU.mult)
-            h_q[b, half] = quantise("h%d%d" % (b, half), staged, COLS)
+                nc.scalar.activation(cut[:, t, :], bank[:], ACT.Tanh, bias=bcut_rows[:, b, t : t + 1])
+            staged = values_staged()
+            for c0 in range(0, HALF, piece):
+                part = slice(c0, c0 + piece)
+                nc.vector.tensor_tensor(
+                    woven(staged[:, : PACK * piece]), by_lines(cut[:, :, part]),
+                    by_lines(response[b, half][:, :, part]), ALU.mult,
+                )
+                h_mx[b, half * HALF + c0] = quantise("h%d_%d" % (b, half * HALF + c0), staged, piece)
 
-        wret_q = {}
-        cut_features(0, 0, lambda t: t)
-        wcut_q[0, 1] = prepare_wcut(0, 1, True)
-        wcut_q[1, 1] = prepare_wcut(1, 1, False)
-        cut_features(0, 1, lambda t: PACK + t)
-        cut_features(1, 0, lambda t: t % 3)
-        wret_q[0] = prepare_wret(0, True)
-        cut_features(1, 1, lambda t: (PACK + t) % 3)
-        wret_q[1] = prepare_wret(1, False)
+        def reading_pass(bank, weights, values, nt, skip, width, start, stop):
+            rows = slice(P * nt, P * (nt + 1))
+            tokens = slice(skip, skip + width)
+            nc.tensor.matmul_mx(
+                out=banks[bank][:, :width],
+                lhsT=weights[0][:, rows].bitcast(E4M3), lhsT_scale=weights[1][:, rows],
+                rhs=values[0][:, tokens].bitcast(E4M3), rhs_scale=values[1][:, tokens],
+                start=start, stop=stop,
+            )
 
-        def readings(half, bank_order):
+        def open_readings(j0, width, bank_order, tiles):
+            half, skip = divmod(j0, HALF)
+            for b in range(r_blocks):
+                wref_mx = (wref_codes[b], wref_planes[4 * b :, :])
+                for nt in tiles:
+                    reading_pass(bank_order[nt], wref_mx, response_mx[b, half], nt, skip, width, b == 0, False)
+            for nt in tiles:
+                reading_pass(bank_order[nt], wret_mx[0], h_mx[0, half * HALF], nt, skip, width, False, False)
+
+        def close_readings(j0, width, bank_order):
             for nt in range(n_tiles):
-                bank = banks[bank_order[nt]]
-                cols = slice(P * nt, P * (nt + 1))
-                for b in range(r_passes):
-                    codes, plane = b_q[b, half]
-                    nc.tensor.matmul_mx(
-                        out=bank[:],
-                        lhsT=wref_codes[b][:, cols].bitcast(E4M3), lhsT_scale=wref_planes[4 * b :, cols],
-                        rhs=codes[:].bitcast(E4M3), rhs_scale=plane[:],
-                        start=(b == 0), stop=False,
-                    )
-                for b in range(r_passes):
-                    codes, plane = h_q[b, half]
-                    w_codes, w_plane = wret_q[b]
-                    nc.tensor.matmul_mx(
-                        out=bank[:],
-                        lhsT=w_codes[:, cols].bitcast(E4M3), lhsT_scale=w_plane[:, cols],
-                        rhs=codes[:].bitcast(E4M3), rhs_scale=plane[:],
-                        start=False, stop=(b == r_passes - 1),
-                    )
-                result = stores.tile([P, COLS], F32, name="result")
-                nc.scalar.activation(result[:], bank[:], ACT.Abs)
-                nc.sync.dma_start(out[cols, half * COLS : (half + 1) * COLS], result[:])
+                reading_pass(bank_order[nt], wret_mx[1], h_mx[1, j0], nt, 0, width, False, True)
 
-        readings(0, [3, 4, 5, 6, 7])
-        readings(1, [2, 0, 1, 3, 4])
+        def hand_out(j0, width, bank_order):
+            for nt in range(n_tiles):
+                result = keep("result%d_%d" % (j0, nt), width, F32)
+                nc.scalar.activation(result[:], banks[bank_order[nt]][:, :width], ACT.Abs)
+                nc.sync.dma_start(out[P * nt : P * (nt + 1), j0 : j0 + width], result[:])
+
+        first_banks, second_banks, third_banks = [3, 4, 5, 6, 7], [2, 0, 1, 3, 4], [5, 6, 7, 2, 0]
+        free_now, free_later = range(3), range(3, n_tiles)
+        second, third = HALF, HALF + QUARTER
+
+        cut_features(0, 0, [0, 1, 2, 3], "cut_first", HALF)
+        for a in range(k_passes):
+            wcut_mx[a, 1] = prepare_wcut(a, 1, nc.scalar.copy)
+        wret_mx = [prepare_wret(b) for b in range(r_blocks)]
+        cut_features(1, 0, [4, 5, 6, 7], "tab_codes0", HALF)
+        cut_features(0, 1, [0, 1, 2, 0], "wcut_raw00", HALF)
+        open_readings(0, HALF, first_banks, range(n_tiles))
+        close_readings(0, HALF, first_banks)
+        cut_features(1, 1, [1, 2, 0, 1], "wcut_raw10", QUARTER)
+        open_readings(second, QUARTER, second_banks, free_now)
+        hand_out(0, HALF, first_banks)
+        open_readings(second, QUARTER, second_banks, free_later)
+        open_readings(third, QUARTER, third_banks, free_now)
+        close_readings(second, QUARTER, second_banks)
+        hand_out(second, QUARTER, second_banks)
+        open_readings(third, QUARTER, third_banks, free_later)
+        close_readings(third, QUARTER, third_banks)
+        hand_out(third, QUARTER, third_banks)

@@ -36,11 +36,16 @@ def tile_list_light_return_audit_kernel(
 
     with ExitStack() as ctx:
         held = ctx.enter_context(tc.tile_pool(name="held", bufs=1))
-        ring = ctx.enter_context(tc.tile_pool(name="ring", bufs=2))
+        values_ring = ctx.enter_context(tc.tile_pool(name="values_ring", bufs=2))
+        wcut_ring = ctx.enter_context(tc.tile_pool(name="wcut_ring", bufs=2))
+        homes = {}
+        for home in ("tab_codes0", "tab_codes1", "wcut_raw00", "wcut_raw10"):
+            homes[home] = ctx.enter_context(tc.tile_pool(name="home_" + home, bufs=1))
+        stores = ctx.enter_context(tc.tile_pool(name="stores", bufs=1))
         psum = ctx.enter_context(tc.psum_pool(name="psum", bufs=1))
 
         def keep(name, width, dtype):
-            return held.tile([P, width], dtype, name=name, align_bytes=64)
+            return homes.get(name, held).tile([P, width], dtype, name=name, align_bytes=64)
 
         banks = [psum.tile([P, HALF], F32, name="bank%d" % i) for i in range(BANKS)]
         offsets = held.tile([P, S // LIST_ROWS], U16, name="offsets")
@@ -59,7 +64,7 @@ def tile_list_light_return_audit_kernel(
                 )
 
         def load_rows(name, rows):
-            raw = held.tile([P, PACK, rows.shape[1]], F32, name=name, align_bytes=64)
+            raw = homes.get(name, held).tile([P, PACK, rows.shape[1]], F32, name=name, align_bytes=64)
             nc.sync.dma_start(raw[:], rows.rearrange("(p j) c -> p j c", j=PACK))
             return raw
 
@@ -79,11 +84,6 @@ def tile_list_light_return_audit_kernel(
         for plane in (xs_plane, tab_planes, wref_planes):
             nc.vector.memset(plane[:].bitcast(I32), 0)
 
-        warm_in = keep("warm_in", 1, F32)
-        warm_out = keep("warm_out", 1, F32)
-        nc.vector.memset(warm_in[:], 0.0)
-        nc.scalar.activation(warm_out[:], warm_in[:], ACT.Tanh)
-
         wscan_raw = keep("wscan_raw", 2 * H, U8)
         nc.sync.dma_start(wscan_raw[:].bitcast(I32), wscan_words[0].bitcast(I32))
         load_planes(wscan_plane_raw, wscan_scales)
@@ -99,9 +99,9 @@ def tile_list_light_return_audit_kernel(
         bcut_rows = load_bias("bcut_rows", bcut)
         for a in range(k_passes):
             wcut_raw[a, 1] = load_wcut(a, 1)
-        load_planes(wref_planes, wref_scales)
-        wref_codes = [load_words("wref_codes%d" % b, wref_words[b]) for b in range(r_blocks)]
         wret_raw = [load_rows("wret_raw%d" % b, wret[b * PASS : (b + 1) * PASS, :]) for b in range(r_blocks)]
+        wref_codes = [load_words("wref_codes%d" % b, wref_words[b]) for b in range(r_blocks)]
+        load_planes(wref_planes, wref_scales)
 
         def quantise(name, staged, width):
             codes = keep(name + "_codes", width, U32)
@@ -121,7 +121,7 @@ def tile_list_light_return_audit_kernel(
             return slices.rearrange("p t (c i) -> p c t i", i=LINE)
 
         def prepare_wcut(a, b, copy):
-            staged = ring.tile([P, PACK * PASS], BF16, name="wcut_staged", align_bytes=64)
+            staged = wcut_ring.tile([P, PACK * PASS], BF16, name="wcut_staged", align_bytes=64)
             copy(
                 staged[:].rearrange("p (t m j) -> p m j t", t=PACK, j=PACK),
                 wcut_raw[a, b][:].rearrange("p j (m t) -> p m j t", t=PACK),
@@ -134,7 +134,7 @@ def tile_list_light_return_audit_kernel(
             return quantise("wret%d" % b, staged, N)
 
         def values_staged():
-            return ring.tile([P, PACK * HALF], BF16, name="values_staged", align_bytes=64)
+            return values_ring.tile([P, PACK * HALF], BF16, name="values_staged", align_bytes=64)
 
         wcut_mx = {(0, 0): prepare_wcut(0, 0, nc.vector.tensor_copy)}
 
@@ -170,8 +170,8 @@ def tile_list_light_return_audit_kernel(
                 nc.scalar.activation(values[:, t, :], bank[:], ACT.Abs, bias=bscan_rows[:, b, t : t + 1])
             response[b, half] = values
 
-        def quantise_response(b, half, staged, copy):
-            copy(woven(staged[:]), by_lines(response[b, half][:]))
+        def quantise_response(b, half, staged):
+            nc.vector.tensor_copy(woven(staged[:]), by_lines(response[b, half][:]))
             response_mx[b, half] = quantise("response%d%d" % (b, half), staged, HALF)
 
         for half in range(halves):
@@ -191,16 +191,20 @@ def tile_list_light_return_audit_kernel(
         v_codes = [gather("v_codes0", tab_codes[0], U32, S), gather("v_codes1", tab_codes[1], U32, HALF)]
 
         for half in range(halves):
-            quantise_response(0, half, values_staged(), nc.vector.tensor_copy)
-        quantise_response(1, 0, values_staged(), nc.scalar.copy)
-        last_staged = held.tile([P, PACK * HALF], BF16, name="last_staged", tag="tab_codes1", align_bytes=64)
-        quantise_response(1, 1, last_staged, nc.vector.tensor_copy)
+            quantise_response(0, half, values_staged())
+        quantise_response(1, 0, values_staged())
+        last_staged = homes["tab_codes1"].tile(
+            [P, PACK * HALF], BF16, name="last_staged", tag="tab_codes1", align_bytes=64
+        )
+        quantise_response(1, 1, last_staged)
 
         h_mx = {}
 
         def cut_features(b, half, bank_order, home, piece):
             tokens = slice(half * HALF, (half + 1) * HALF)
-            cut = held.tile([P, PACK, HALF], F32, name="cut%d%d" % (b, half), tag=home, align_bytes=64)
+            cut = homes.get(home, held).tile(
+                [P, PACK, HALF], F32, name="cut%d%d" % (b, half), tag=home, align_bytes=64
+            )
             for t in range(PACK):
                 bank = banks[bank_order[t]]
                 columns = slice(P * t, P * (t + 1))
@@ -232,28 +236,23 @@ def tile_list_light_return_audit_kernel(
                 start=start, stop=stop,
             )
 
-        def open_readings(j0, width, bank_order, tiles):
+        def readings(j0, width, bank_order):
             half, skip = divmod(j0, HALF)
-            for b in range(r_blocks):
-                wref_mx = (wref_codes[b], wref_planes[4 * b :, :])
-                for nt in tiles:
-                    reading_pass(bank_order[nt], wref_mx, response_mx[b, half], nt, skip, width, b == 0, False)
-            for nt in tiles:
-                reading_pass(bank_order[nt], wret_mx[0], h_mx[0, half * HALF], nt, skip, width, False, False)
-
-        def close_readings(j0, width, bank_order):
             for nt in range(n_tiles):
-                reading_pass(bank_order[nt], wret_mx[1], h_mx[1, j0], nt, 0, width, False, True)
+                bank = bank_order[nt]
+                for b in range(r_blocks):
+                    wref_mx = (wref_codes[b], wref_planes[4 * b :, :])
+                    reading_pass(bank, wref_mx, response_mx[b, half], nt, skip, width, b == 0, False)
+                reading_pass(bank, wret_mx[0], h_mx[0, half * HALF], nt, skip, width, False, False)
+                reading_pass(bank, wret_mx[1], h_mx[1, j0], nt, 0, width, False, True)
 
         def hand_out(j0, width, bank_order):
             for nt in range(n_tiles):
-                result = keep("result%d_%d" % (j0, nt), width, F32)
+                result = stores.tile([P, width], F32, name="result%d_%d" % (j0, nt))
                 nc.scalar.activation(result[:], banks[bank_order[nt]][:, :width], ACT.Abs)
                 nc.sync.dma_start(out[P * nt : P * (nt + 1), j0 : j0 + width], result[:])
 
         first_banks, second_banks, third_banks = [3, 4, 5, 6, 7], [2, 0, 1, 3, 4], [5, 6, 7, 2, 0]
-        free_now, free_later = range(3), range(3, n_tiles)
-        second, third = HALF, HALF + QUARTER
 
         cut_features(0, 0, [0, 1, 2, 3], "cut_first", HALF)
         for a in range(k_passes):
@@ -261,15 +260,9 @@ def tile_list_light_return_audit_kernel(
         wret_mx = [prepare_wret(b) for b in range(r_blocks)]
         cut_features(1, 0, [4, 5, 6, 7], "tab_codes0", HALF)
         cut_features(0, 1, [0, 1, 2, 0], "wcut_raw00", HALF)
-        open_readings(0, HALF, first_banks, range(n_tiles))
-        close_readings(0, HALF, first_banks)
+        readings(0, HALF, first_banks)
         cut_features(1, 1, [1, 2, 0, 1], "wcut_raw10", QUARTER)
-        open_readings(second, QUARTER, second_banks, free_now)
         hand_out(0, HALF, first_banks)
-        open_readings(second, QUARTER, second_banks, free_later)
-        open_readings(third, QUARTER, third_banks, free_now)
-        close_readings(second, QUARTER, second_banks)
-        hand_out(second, QUARTER, second_banks)
-        open_readings(third, QUARTER, third_banks, free_later)
-        close_readings(third, QUARTER, third_banks)
-        hand_out(third, QUARTER, third_banks)
+        for j0, bank_order in ((HALF, second_banks), (HALF + QUARTER, third_banks)):
+            readings(j0, QUARTER, bank_order)
+            hand_out(j0, QUARTER, bank_order)

from contextlib import ExitStack

import concourse.mybir as mybir

K, K2, H, N, T, S = 1024, 512, 1024, 640, 4096, 1024
FLOPS = 2 * S * (K * H + K2 * H + 2 * H * N)

F32 = mybir.dt.float32
BF16 = mybir.dt.bfloat16
I32 = mybir.dt.int32
U32 = mybir.dt.uint32
U16 = mybir.dt.uint16
U8 = mybir.dt.uint8
E4M3 = mybir.dt.float8_e4m3fn_x4
E2M1 = mybir.dt.float4_e2m1fn_x4
ACT = mybir.ActivationFunctionType
ALU = mybir.AluOpType

P = 128
PACK = 4
PASS = P * PACK
QUADS = 4
HALF = 512
QUARTER = HALF // 2
BANKS = 8
LINE = 4
LIST_ROWS = 16


def tile_list_light_return_audit_kernel(
    tc, tab_words, tab_scales, offs, xs_words, xs_scales, wcut, bcut,
    wscan_words, wscan_scales, bscan, wret, wref_words, wref_scales, out,
):
    nc = tc.nc
    k_passes, r_blocks, halves, n_tiles = K // PASS, H // PASS, S // HALF, N // P

    with ExitStack() as ctx:
        held = ctx.enter_context(tc.tile_pool(name="held", bufs=1))
        values_ring = ctx.enter_context(tc.tile_pool(name="values_ring", bufs=2))
        wcut_ring = ctx.enter_context(tc.tile_pool(name="wcut_ring", bufs=2))
        homes = {}
        for home in ("tab_codes0", "tab_codes1", "wcut_raw00", "wcut_raw10"):
            homes[home] = ctx.enter_context(tc.tile_pool(name="home_" + home, bufs=1))
        stores = ctx.enter_context(tc.tile_pool(name="stores", bufs=1))
        psum = ctx.enter_context(tc.psum_pool(name="psum", bufs=1))

        def keep(name, width, dtype):
            return homes.get(name, held).tile([P, width], dtype, name=name, align_bytes=64)

        banks = [psum.tile([P, HALF], F32, name="bank%d" % i) for i in range(BANKS)]
        offsets = held.tile([P, S // LIST_ROWS], U16, name="offsets")

        def load_words(name, words):
            tile = keep(name, words.shape[1], U32)
            nc.sync.dma_start(tile[:].bitcast(I32), words.rearrange("p n t -> p (n t)").bitcast(I32))
            return tile

        def load_planes(tile, scales):
            passes = scales.shape[0]
            for q in range(QUADS):
                nc.sync.dma_start(
                    tile[32 * q : 32 * q + 4 * passes, :].bitcast(I32),
                    scales[:, 4 * q : 4 * q + 4, :].bitcast(I32),
                )

        def load_rows(name, rows):
            raw = homes.get(name, held).tile([P, PACK, rows.shape[1]], F32, name=name, align_bytes=64)
            nc.sync.dma_start(raw[:], rows.rearrange("(p j) c -> p j c", j=PACK))
            return raw

        def load_wcut(a, b):
            return load_rows("wcut_raw%d%d" % (a, b), wcut[a * PASS : (a + 1) * PASS, b * PASS : (b + 1) * PASS])

        def load_bias(name, vec):
            tile = held.tile([P, r_blocks, PACK], F32, name=name, align_bytes=64)
            nc.sync.dma_start(tile[:], vec.rearrange("(b p t) -> p b t", b=r_blocks, t=PACK))
            return tile

        wscan_plane_raw = keep("wscan_plane_raw", H, U8)
        xs_plane = keep("xs_plane", S, U8)
        tab_planes = keep("tab_planes", T, U8)
        wref_planes = keep("wref_planes", N, U8)
        nc.gpsimd.memset(wscan_plane_raw[:].bitcast(I32), 0)
        for plane in (xs_plane, tab_planes, wref_planes):
            nc.vector.memset(plane[:].bitcast(I32), 0)

        wscan_raw = keep("wscan_raw", 2 * H, U8)
        nc.sync.dma_start(wscan_raw[:].bitcast(I32), wscan_words[0].bitcast(I32))
        load_planes(wscan_plane_raw, wscan_scales)
        xs_codes = load_words("xs_codes", xs_words[0])
        load_planes(xs_plane, xs_scales)
        bscan_rows = load_bias("bscan_rows", bscan)
        wcut_raw = {(0, 0): load_wcut(0, 0)}
        load_planes(tab_planes, tab_scales)
        nc.sync.dma_start(offsets[:], offs)
        tab_codes = [load_words("tab_codes0", tab_words[0])]
        wcut_raw[1, 0] = load_wcut(1, 0)
        tab_codes.append(load_words("tab_codes1", tab_words[1]))
        bcut_rows = load_bias("bcut_rows", bcut)
        for a in range(k_passes):
            wcut_raw[a, 1] = load_wcut(a, 1)
        wret_raw = [load_rows("wret_raw%d" % b, wret[b * PASS : (b + 1) * PASS, :]) for b in range(r_blocks)]
        wref_codes = [load_words("wref_codes%d" % b, wref_words[b]) for b in range(r_blocks)]
        load_planes(wref_planes, wref_scales)

        def quantise(name, staged, width):
            codes = keep(name + "_codes", width, U32)
            plane = keep(name + "_plane", width, U8)
            for c0 in range(0, width, HALF):
                c1 = min(c0 + HALF, width)
                nc.vector.quantize_mx(
                    out=codes[:, c0:c1].bitcast(E4M3), scales=plane[:, c0:c1],
                    in_=staged[:, PACK * c0 : PACK * c1],
                )
            return codes, plane

        def woven(staged):
            return staged.rearrange("p (c i t) -> p c t i", i=LINE, t=PACK)

        def by_lines(slices):
            return slices.rearrange("p t (c i) -> p c t i", i=LINE)

        def prepare_wcut(a, b, copy):
            staged = wcut_ring.tile([P, PACK * PASS], BF16, name="wcut_staged", align_bytes=64)
            copy(
                staged[:].rearrange("p (t m j) -> p m j t", t=PACK, j=PACK),
                wcut_raw[a, b][:].rearrange("p j (m t) -> p m j t", t=PACK),
            )
            return quantise("wcut%d%d" % (a, b), staged, PASS)

        def prepare_wret(b):
            staged = keep("wret_staged%d" % b, PACK * N, BF16)
            nc.vector.tensor_scalar_mul(woven(staged[:]), by_lines(wret_raw[b][:]), -1.0)
            return quantise("wret%d" % b, staged, N)

        def values_staged():
            return values_ring.tile([P, PACK * HALF], BF16, name="values_staged", align_bytes=64)

        wcut_mx = {(0, 0): prepare_wcut(0, 0, nc.vector.tensor_copy)}

        wscan_codes, wscan_plane = [], []
        for b in range(r_blocks):
            codes = keep("wscan_codes%d" % b, 2 * PASS, U8)
            plane = keep("wscan_plane%d" % b, PASS, U8)
            nc.vector.tensor_copy(
                codes[:].rearrange("p (t m e) -> p t m e", t=PACK, e=2),
                wscan_raw[:, 2 * PASS * b : 2 * PASS * (b + 1)].rearrange("p (m t e) -> p t m e", t=PACK, e=2),
            )
            nc.vector.tensor_copy(
                plane[:].rearrange("p (t m) -> p t m", t=PACK),
                wscan_plane_raw[:, PASS * b : PASS * (b + 1)].rearrange("p (m t) -> p t m", t=PACK),
            )
            wscan_codes.append(codes)
            wscan_plane.append(plane)

        response, response_mx = {}, {}

        def scan_response(b, half):
            tokens = slice(half * HALF, (half + 1) * HALF)
            values = held.tile([P, PACK, HALF], F32, name="response%d%d" % (b, half), align_bytes=64)
            for t in range(PACK):
                bank = banks[PACK * half + t]
                nc.tensor.matmul_mx(
                    out=bank[:],
                    lhsT=wscan_codes[b][:, 2 * P * t : 2 * P * (t + 1)].bitcast(E2M1),
                    lhsT_scale=wscan_plane[b][:, P * t : P * (t + 1)],
                    rhs=xs_codes[:, tokens].bitcast(E4M3), rhs_scale=xs_plane[:, tokens],
                    start=True, stop=True,
                )
                nc.scalar.activation(values[:, t, :], bank[:], ACT.Abs, bias=bscan_rows[:, b, t : t + 1])
            response[b, half] = values

        def quantise_response(b, half, staged):
            nc.vector.tensor_copy(woven(staged[:]), by_lines(response[b, half][:]))
            response_mx[b, half] = quantise("response%d%d" % (b, half), staged, HALF)

        for half in range(halves):
            scan_response(0, half)
        wcut_mx[1, 0] = prepare_wcut(1, 0, nc.scalar.copy)
        for half in range(halves):
            scan_response(1, half)

        def gather(name, window, dtype, piece):
            picked = keep(name, S, dtype)
            for j0 in range(0, S, piece):
                entries = offsets[:, j0 // LIST_ROWS : (j0 + piece) // LIST_ROWS]
                nc.vector.tensor_copy(picked[:, j0 : j0 + piece], window[:].indirect(entries))
            return picked

        v_planes = gather("v_planes", tab_planes, U8, S)
        v_codes = [gather("v_codes0", tab_codes[0], U32, S), gather("v_codes1", tab_codes[1], U32, HALF)]

        for half in range(halves):
            quantise_response(0, half, values_staged())
        quantise_response(1, 0, values_staged())
        last_staged = homes["tab_codes1"].tile(
            [P, PACK * HALF], BF16, name="last_staged", tag="tab_codes1", align_bytes=64
        )
        quantise_response(1, 1, last_staged)

        h_mx = {}

        def cut_features(b, half, bank_order, home, piece):
            tokens = slice(half * HALF, (half + 1) * HALF)
            cut = homes.get(home, held).tile(
                [P, PACK, HALF], F32, name="cut%d%d" % (b, half), tag=home, align_bytes=64
            )
            for t in range(PACK):
                bank = banks[bank_order[t]]
                columns = slice(P * t, P * (t + 1))
                for a in range(k_passes):
                    codes, plane = wcut_mx[a, b]
                    nc.tensor.matmul_mx(
                        out=bank[:],
                        lhsT=codes[:, columns].bitcast(E4M3), lhsT_scale=plane[:, columns],
                        rhs=v_codes[a][:, tokens].bitcast(E4M3), rhs_scale=v_planes[4 * a :, tokens],
                        start=(a == 0), stop=(a == k_passes - 1),
                    )
                nc.scalar.activation(cut[:, t, :], bank[:], ACT.Tanh, bias=bcut_rows[:, b, t : t + 1])
            staged = values_staged()
            for c0 in range(0, HALF, piece):
                part = slice(c0, c0 + piece)
                nc.vector.tensor_tensor(
                    woven(staged[:, : PACK * piece]), by_lines(cut[:, :, part]),
                    by_lines(response[b, half][:, :, part]), ALU.mult,
                )
                h_mx[b, half * HALF + c0] = quantise("h%d_%d" % (b, half * HALF + c0), staged, piece)

        def reading_pass(bank, weights, values, nt, skip, width, start, stop):
            rows = slice(P * nt, P * (nt + 1))
            tokens = slice(skip, skip + width)
            nc.tensor.matmul_mx(
                out=banks[bank][:, :width],
                lhsT=weights[0][:, rows].bitcast(E4M3), lhsT_scale=weights[1][:, rows],
                rhs=values[0][:, tokens].bitcast(E4M3), rhs_scale=values[1][:, tokens],
                start=start, stop=stop,
            )

        def readings(j0, width, bank_order):
            half, skip = divmod(j0, HALF)
            for nt in range(n_tiles):
                bank = bank_order[nt]
                for b in range(r_blocks):
                    wref_mx = (wref_codes[b], wref_planes[4 * b :, :])
                    reading_pass(bank, wref_mx, response_mx[b, half], nt, skip, width, b == 0, False)
                reading_pass(bank, wret_mx[0], h_mx[0, half * HALF], nt, skip, width, False, False)
                reading_pass(bank, wret_mx[1], h_mx[1, j0], nt, 0, width, False, True)

        def hand_out(j0, width, bank_order):
            for nt in range(n_tiles):
                result = stores.tile([P, width], F32, name="result%d_%d" % (j0, nt))
                nc.scalar.activation(result[:], banks[bank_order[nt]][:, :width], ACT.Abs)
                nc.sync.dma_start(out[P * nt : P * (nt + 1), j0 : j0 + width], result[:])

        first_banks, second_banks, third_banks = [3, 4, 5, 6, 7], [2, 0, 1, 3, 4], [5, 6, 7, 2, 0]

        cut_features(0, 0, [0, 1, 2, 3], "cut_first", HALF)
        for a in range(k_passes):
            wcut_mx[a, 1] = prepare_wcut(a, 1, nc.scalar.copy)
        wret_mx = [prepare_wret(b) for b in range(r_blocks)]
        cut_features(1, 0, [4, 5, 6, 7], "tab_codes0", HALF)
        cut_features(0, 1, [0, 1, 2, 0], "wcut_raw00", HALF)
        readings(0, HALF, first_banks)
        cut_features(1, 1, [1, 2, 0, 1], "wcut_raw10", QUARTER)
        hand_out(0, HALF, first_banks)
        for j0, bank_order in ((HALF, second_banks), (HALF + QUARTER, third_banks)):
            readings(j0, QUARTER, bank_order)
            hand_out(j0, QUARTER, bank_order)
